import numpy as np
import ml_dtypes


def mxq(x, axis, fmt="e4m3"):
    dtype, down = {"e4m3": (ml_dtypes.float8_e4m3fn, 7), "e5m2": (ml_dtypes.float8_e5m2, 14)}[fmt]
    v = np.moveaxis(np.asarray(x, np.float32).astype(ml_dtypes.bfloat16).astype(np.float64), axis, -1)
    blocks = v.reshape(v.shape[:-1] + (-1, 32))
    amax = np.abs(blocks).max(-1, keepdims=True)
    byte = np.maximum(np.where(amax > 0, np.frexp(amax)[1] - 1 + 127, 0) - down, 1)
    scale = np.exp2(byte - 127.0)
    codes = (blocks / scale).astype(np.float32).astype(dtype).astype(np.float64)
    return np.moveaxis((codes * scale).reshape(v.shape), -1, axis)


WIDE = False


def mx_kscale(k):
    if not WIDE:
        return np.ones(k)
    levels = np.array([10, -10, 5, -5, 0])
    if k % 512:
        return np.exp2(np.random.permutation(np.resize(levels, k // 32))).repeat(32)
    a = np.empty((k // 512, 16))
    for p in range(k // 512):
        a[p, :8] = np.random.permutation(np.resize(levels, 8))
        for g in range(8):
            far = levels[np.abs(levels - a[p, g]) >= 10]
            a[p, g + 8] = far[np.random.randint(len(far))]
    return np.exp2(a.ravel()).repeat(32)


def f64(x):
    return np.asarray(x).astype(np.float64)


def striped8(idx):
    return np.asarray(idx).reshape(8, -1, 16).transpose(0, 2, 1).reshape(128, -1).astype(np.uint16)


def unstriped8(offs):
    return offs.reshape(8, 16, -1).transpose(0, 2, 1).reshape(8, -1).astype(np.int64)


def pick8(x, idx, run):
    r = np.arange(len(x))
    return x[r[:, None], idx[r % (8 * run) // run]]


E2M1 = np.array([0.0, 0.5, 1.0, 1.5, 2.0, 3.0, 4.0, 6.0, -0.0, -0.5, -1.0, -1.5, -2.0, -3.0, -4.0, -6.0])


def pack_weight(w, fmt):
    k, n = w.shape
    w = f64(np.asarray(w, np.float32).astype(ml_dtypes.bfloat16)).reshape(k // 32, 32, n)
    amax = np.abs(w).max(1)
    if fmt == "e4m3":
        byte = np.frexp(amax)[1] - 1 + 127 - 7
    else:
        mant, ex = np.frexp(amax / 6.0)
        byte = np.where(mant > 0.5, ex, ex - 1) + 127
    byte = np.clip(np.where(amax > 0, byte, 1), 1, 254)
    scaled = (w * np.exp2(127.0 - byte)[:, None, :]).reshape(k, n).astype(np.float32)
    by_word = np.ascontiguousarray(scaled.reshape(k // 512, 128, 4, n).transpose(0, 1, 3, 2))
    if fmt == "e4m3":
        words = by_word.astype(ml_dtypes.float8_e4m3fn).view(np.uint8)
    else:
        c = by_word.astype(ml_dtypes.float4_e2m1fn).view(np.uint8) & 0xF
        words = (c[..., 0::2] | (c[..., 1::2] << 4)).reshape(k // 512, 128, 2 * n)
    return np.ascontiguousarray(words), np.ascontiguousarray(byte.astype(np.uint8).reshape(k // 512, 16, n))


def unpack_weight(words, scales, fmt):
    g, _, n = scales.shape
    words = np.ascontiguousarray(words).reshape(g, 128, n, -1)
    if fmt == "e4m3":
        vals = words.view(ml_dtypes.float8_e4m3fn).astype(np.float64)
    else:
        nib = np.empty((g, 128, n, 4), np.uint8)
        nib[..., 0::2] = words & 0xF
        nib[..., 1::2] = words >> 4
        vals = E2M1[nib]
    vals = vals * np.repeat(np.exp2(scales.astype(np.float64) - 127.0), 8, axis=1)[..., None]
    return vals.transpose(0, 1, 3, 2).reshape(g * 512, n)


D, T, U, X, I, J, Q, E = 512, 1024, 1024, 1024, 512, 256, 512, 256


def setup_inputs():
    n = np.random.standard_normal
    idx = np.stack([np.random.permutation(T)[:J] for _ in range(8)])
    idx2 = np.stack([np.random.permutation(U)[:J] for _ in range(8)])
    idx3 = np.stack([np.random.permutation(X)[:I] for _ in range(8)])
    idx4 = np.stack([np.random.permutation(X)[:I] for _ in range(8)])
    idx5 = np.stack([np.random.permutation(X)[:I] for _ in range(8)])
    fd = mx_kscale(D)
    fq = mx_kscale(Q)
    keysp = pack_weight(n((D, T)) / fd[:, None], "e2m1")
    notesp = pack_weight(n((D, U)) / fd[:, None], "e4m3")
    usersp = pack_weight(n((D, X)) / fd[:, None], "e4m3")
    mixp = pack_weight(n((Q, E)) * 1.0 / np.sqrt(Q) / fq[:, None], "e4m3")
    return {
        "query": (n((D, Q)) * 1.0 / np.sqrt(D) * fd[:, None]).astype(np.float32),
        "query2": (n((D, Q)) * 1.0 / np.sqrt(D) * fd[:, None]).astype(np.float32),
        "keys_words": keysp[0],
        "keys_scales": keysp[1],
        "notes_words": notesp[0],
        "notes_scales": notesp[1],
        "users_words": usersp[0],
        "users_scales": usersp[1],
        "rowf": (np.random.uniform(0.5, 2.0, (Q, 1)) * fq[:, None]).astype(np.float32),
        "mix_words": mixp[0],
        "mix_scales": mixp[1],
        "offs": striped8(idx),
        "offs2": striped8(idx2),
        "offs3": striped8(idx3),
        "offs4": striped8(idx4),
        "offs5": striped8(idx5),
    }


def reference(query, query2, keys_words, keys_scales, notes_words, notes_scales, users_words, users_scales, rowf, mix_words, mix_scales, offs, offs2, offs3, offs4, offs5):
    idx = unstriped8(offs)
    idx2 = unstriped8(offs2)
    idx3 = unstriped8(offs3)
    idx4 = unstriped8(offs4)
    idx5 = unstriped8(offs5)
    keysu = unpack_weight(keys_words, keys_scales, "e2m1")
    notesu = unpack_weight(notes_words, notes_scales, "e4m3")
    usersu = unpack_weight(users_words, users_scales, "e4m3")
    mixu = unpack_weight(mix_words, mix_scales, "e4m3")
    queryq = mxq(f64(query), 0, "e4m3")
    a = queryq.T @ keysu
    b = queryq.T @ notesu
    query2q = mxq(f64(query2), 0, "e4m3")
    c0 = query2q.T @ usersu
    w = np.concatenate([pick8(a, idx, 64), pick8(b, idx2, 64)], axis=1)
    v = np.maximum(w, pick8(c0, idx3, 64))
    f1 = np.zeros((Q, X))
    f1[np.arange(Q)[:, None], idx4[np.arange(Q) % 512 // 64]] = v
    cc = c0 + f1
    g = pick8(cc, idx5, 64)
    gw = g * f64(rowf)
    gwq = mxq(gw, 0, "e4m3")
    y = mixu.T @ gwq
    return y

@@ -1,0 +1,201 @@
+from contextlib import ExitStack
+
+import concourse.mybir as mybir
+
+F32 = mybir.dt.float32
+BF16 = mybir.dt.bfloat16
+I32 = mybir.dt.int32
+U32 = mybir.dt.uint32
+U16 = mybir.dt.uint16
+U8 = mybir.dt.uint8
+FP8X4 = mybir.dt.float8_e4m3fn_x4
+FP4X4 = mybir.dt.float4_e2m1fn_x4
+COPY = mybir.ActivationFunctionType.Copy
+ALU = mybir.AluOpType
+
+P = 128
+PACK = 4
+D, Q, COLS, SLOTS, E = 512, 512, 1024, 512, 256
+HALF = SLOTS // 2
+BANK = 512
+CHUNKS = 2
+LIST = 16
+
+FLOPS = 2 * D * Q * COLS * 3 + 2 * Q * E * SLOTS
+
+
+def tile_attend_joinedbest_threeq_mixed_kernel(
+    tc, query, query2, keys_words, keys_scales, notes_words, notes_scales, users_words, users_scales,
+    rowf, mix_words, mix_scales, offs, offs2, offs3, offs4, offs5, out,
+):
+    nc = tc.nc
+    with ExitStack() as ctx:
+        keep = ctx.enter_context(tc.tile_pool(name="keep", bufs=1))
+        psum = ctx.enter_context(tc.psum_pool(name="psum", bufs=4))
+
+        def load_query(name, src):
+            width = Q // CHUNKS
+            rows = src.rearrange("(p j) q -> p j q", j=PACK)
+            raws = []
+            for c in range(CHUNKS):
+                raw = keep.tile([P, PACK, width], F32, name="%s_raw%d" % (name, c))
+                nc.sync.dma_start(raw[:], rows[:, :, c * width : (c + 1) * width])
+                raws.append(raw)
+            return raws
+
+        def load_scales(name, src, width):
+            plane = keep.tile([P, width], U8, name=name, align_bytes=64)
+            rows = src[0].rearrange("(g r) n -> r g n", r=PACK)
+            for r in range(PACK):
+                nc.sync.dma_start(plane[r:P:32, :].bitcast(I32), rows[r].bitcast(I32))
+            return plane
+
+        def load_words(name, src, nbytes):
+            words = keep.tile([P, nbytes], U8, name=name, align_bytes=64)
+            nc.sync.dma_start(words[:].bitcast(I32), src.bitcast(I32))
+            return words
+
+        def load_list(name, src, n):
+            lst = keep.tile([P, n // LIST], U16, name=name)
+            nc.sync.dma_start(lst[:], src)
+            return lst
+
+        flat = "p n t -> p (n t)"
+        q_raw = load_query("q", query)
+        key_sc = load_scales("key_sc", keys_scales, COLS)
+        key_w = load_words("key_w", keys_words[0], 2 * COLS)
+        l_a = load_list("l_a", offs, HALF)
+        q2_raw = load_query("q2", query2)
+        user_sc = load_scales("user_sc", users_scales, COLS)
+        user_w = load_words("user_w", users_words[0].rearrange(flat), 4 * COLS)
+        l_c = load_list("l_c", offs3, SLOTS)
+        l_put = load_list("l_put", offs4, SLOTS)
+        note_sc = load_scales("note_sc", notes_scales, COLS)
+        note_w = load_words("note_w", notes_words[0].rearrange(flat), 4 * COLS)
+        l_b = load_list("l_b", offs2, HALF)
+        l_g = load_list("l_g", offs5, SLOTS)
+        row_f = keep.tile([P, PACK], F32, name="row_f")
+        nc.sync.dma_start(row_f[:], rowf.rearrange("(p t) o -> p (t o)", t=PACK))
+        mix_w = load_words("mix_w", mix_words[0].rearrange(flat), 4 * E)
+        mix_sc = load_scales("mix_sc", mix_scales, E)
+
+        placed = [keep.tile([P, COLS], F32, name="placed%d" % k) for k in range(2)]
+        for tile in placed:
+            nc.vector.memset(tile[:], 0.0)
+
+        def quantise_query(name, raws):
+            dealt = keep.tile([P, PACK, P, PACK], BF16, name=name + "_dealt", align_bytes=64)
+            codes = keep.tile([P, Q], U32, name=name + "_codes", align_bytes=64)
+            scales = keep.tile([P, Q], U8, name=name + "_scales", align_bytes=64)
+            per = P // CHUNKS
+            for c, raw in enumerate(raws):
+                nc.vector.tensor_copy(
+                    dealt[:, :, c * per : (c + 1) * per, :].rearrange("p t m j -> p m j t"),
+                    raw[:].rearrange("p j (m t) -> p m j t", t=PACK),
+                )
+            for t in range(PACK):
+                cols = slice(t * P, (t + 1) * P)
+                nc.vector.quantize_mx(
+                    out=codes[:, cols].bitcast(FP8X4), scales=scales[:, cols],
+                    in_=dealt[:, t].rearrange("p m j -> p (m j)"),
+                )
+            return codes, scales
+
+        def scores(name, tag, t, quantised, words, plane, dtype, copiers):
+            codes, scales = quantised
+            cols = slice(t * P, (t + 1) * P)
+            nbytes = words.shape[1] // COLS
+            whole = keep.tile([P, COLS], F32, name="%s%d" % (name, t))
+            for h in range(COLS // BANK):
+                bank = psum.tile([P, BANK], F32, name=tag)
+                nc.tensor.matmul_mx(
+                    out=bank[:], lhsT=codes[:, cols].bitcast(FP8X4), lhsT_scale=scales[:, cols],
+                    rhs=words[:, h * BANK * nbytes : (h + 1) * BANK * nbytes].bitcast(dtype),
+                    rhs_scale=plane[:, h * BANK : (h + 1) * BANK], start=True, stop=True,
+                )
+                copiers[h](whole[:, h * BANK : (h + 1) * BANK], bank[:])
+            return whole
+
+        def part(lst, lo, hi):
+            return lst[:, lo // LIST : hi // LIST]
+
+        def s_gather(dst, window, offsets):
+            nc.scalar.activation(dst, window[:].indirect(offsets), COPY)
+
+        def v_gather(dst, window, offsets):
+            nc.vector.tensor_copy(dst, window[:].indirect(offsets))
+
+        s_copy, v_copy = nc.scalar.copy, nc.vector.tensor_copy
+        w = [keep.tile([P, SLOTS], F32, name="w%d" % t) for t in range(PACK)]
+        c_pick = [keep.tile([P, SLOTS], F32, name="c_pick%d" % t) for t in range(PACK)]
+        v = [keep.tile([P, SLOTS], F32, name="v%d" % t) for t in range(PACK)]
+        cc = [keep.tile([P, COLS], F32, name="cc%d" % t) for t in range(PACK)]
+        g = [keep.tile([P, SLOTS], F32, name="g%d" % t) for t in range(PACK)]
+        gw = keep.tile([P, PACK, SLOTS], BF16, name="gw")
+
+        qq = quantise_query("q", q_raw)
+
+        def tokens(t):
+            a = scores("a", "ab_bank", t, qq, key_w, key_sc, FP4X4, (s_copy, v_copy if t == 0 else s_copy))
+            s_gather(w[t][:, :HALF], a, l_a[:])
+
+        def notes(t):
+            b = scores("b", "ab_bank", t, qq, note_w, note_sc, FP8X4, (s_copy, s_copy))
+            s_gather(w[t][:, HALF:], b, l_b[:])
+
+        def put(t, c0, lo, hi):
+            (v_gather if t == 2 else s_gather)(c_pick[t][:, lo:hi], c0, part(l_c, lo, hi))
+            nc.vector.tensor_tensor(v[t][:, lo:hi], w[t][:, lo:hi], c_pick[t][:, lo:hi], ALU.max)
+            nc.vector.tensor_copy(placed[t % 2][:].indirect(part(l_put, lo, hi)), v[t][:, lo:hi])
+
+        tokens(0)
+        tokens(1)
+        qq2 = quantise_query("q2", q2_raw)
+
+        for t in range(PACK):
+            if t == 0:
+                c0 = scores("c", "c_bank", t, qq2, user_w, user_sc, FP8X4, (s_copy, v_copy))
+                put(t, c0, 0, HALF)
+                notes(t)
+                put(t, c0, HALF, SLOTS)
+            else:
+                if t >= 2:
+                    tokens(t)
+                c0 = scores("c", "c_bank", t, qq2, user_w, user_sc, FP8X4, (s_copy, s_copy))
+                notes(t)
+                put(t, c0, 0, SLOTS)
+            nc.vector.tensor_tensor(cc[t][:], c0[:], placed[t % 2][:], ALU.add)
+
+        last = PACK - 1
+        for t in range(last):
+            s_gather(g[t][:], cc[t], l_g[:])
+            if t < 2:
+                nc.scalar.activation(gw[:, t, :], g[t][:], COPY, scale=row_f[:, t : t + 1])
+            else:
+                nc.vector.tensor_scalar(gw[:, t, :], g[t][:], row_f[:, t : t + 1], None, ALU.mult)
+        s_gather(g[last][:, HALF:], cc[last], part(l_g, HALF, SLOTS))
+        v_gather(g[last][:, :HALF], cc[last], part(l_g, 0, HALF))
+        out_rows = out.rearrange("(u p) i -> p u i", p=P)
+        for h in range(2):
+            slots = slice(h * HALF, (h + 1) * HALF)
+            nc.vector.tensor_scalar(gw[:, last, slots], g[last][:, slots], row_f[:, last : last + 1], None, ALU.mult)
+            woven = keep.tile([P, HALF, PACK], BF16, name="woven%d" % h, align_bytes=64)
+            nc.vector.tensor_copy(
+                woven[:].rearrange("p (c i) t -> p c t i", i=4),
+                gw[:, :, slots].rearrange("p t (c i) -> p c t i", i=4),
+            )
+            gw_codes = keep.tile([P, HALF], U32, name="gw_codes%d" % h, align_bytes=64)
+            gw_scales = keep.tile([P, HALF], U8, name="gw_scales%d" % h, align_bytes=64)
+            nc.vector.quantize_mx(
+                out=gw_codes[:].bitcast(FP8X4), scales=gw_scales[:], in_=woven[:].rearrange("p i t -> p (i t)")
+            )
+            bank = psum.tile([P, BANK], F32, name="c_bank")
+            for u in range(E // P):
+                nc.tensor.matmul_mx(
+                    out=bank[:, u * HALF : (u + 1) * HALF],
+                    lhsT=mix_w[:, u * P * 4 : (u + 1) * P * 4].bitcast(FP8X4), lhsT_scale=mix_sc[:, u * P : (u + 1) * P],
+                    rhs=gw_codes[:].bitcast(FP8X4), rhs_scale=gw_scales[:], start=True, stop=True,
+                )
+            result = keep.tile([P, E // P, HALF], F32, name="result%d" % h)
+            nc.scalar.copy(result[:].rearrange("p u i -> p (u i)"), bank[:])
+            nc.sync.dma_start(out_rows[:, :, slots], result[:])

@@ -18,8 +18,8 @@ PACK = 4
 D, Q, COLS, SLOTS, E = 512, 512, 1024, 512, 256
 HALF = SLOTS // 2
 BANK = 512
-CHUNKS = 2
 LIST = 16
+RING = 4
 
 FLOPS = 2 * D * Q * COLS * 3 + 2 * Q * E * SLOTS
 
@@ -31,23 +31,28 @@ def tile_attend_joinedbest_threeq_mixed_kernel(
     nc = tc.nc
     with ExitStack() as ctx:
         keep = ctx.enter_context(tc.tile_pool(name="keep", bufs=1))
-        psum = ctx.enter_context(tc.psum_pool(name="psum", bufs=4))
+        psum = ctx.enter_context(tc.psum_pool(name="psum", bufs=1))
+        banks = [psum.tile([P, BANK], F32, name="bank%d" % k) for k in range(RING)]
+        used = []
+
+        def next_bank():
+            used.append(1)
+            return banks[(len(used) - 1) % RING]
 
         def load_query(name, src):
-            width = Q // CHUNKS
             rows = src.rearrange("(p j) q -> p j q", j=PACK)
             raws = []
-            for c in range(CHUNKS):
-                raw = keep.tile([P, PACK, width], F32, name="%s_raw%d" % (name, c))
-                nc.sync.dma_start(raw[:], rows[:, :, c * width : (c + 1) * width])
+            for c in range(2):
+                raw = keep.tile([P, 2, Q], F32, name="%s_raw%d" % (name, c))
+                nc.sync.dma_start(raw[:], rows[:, 2 * c : 2 * c + 2, :])
                 raws.append(raw)
             return raws
 
-        def load_scales(name, src, width):
+        def load_scales(name, src, width, queue):
             plane = keep.tile([P, width], U8, name=name, align_bytes=64)
             rows = src[0].rearrange("(g r) n -> r g n", r=PACK)
             for r in range(PACK):
-                nc.sync.dma_start(plane[r:P:32, :].bitcast(I32), rows[r].bitcast(I32))
+                queue.dma_start(plane[r:P:32, :].bitcast(I32), rows[r].bitcast(I32))
             return plane
 
         def load_words(name, src, nbytes):
@@ -62,52 +67,50 @@ def tile_attend_joinedbest_threeq_mixed_kernel(
 
         flat = "p n t -> p (n t)"
         q_raw = load_query("q", query)
-        key_sc = load_scales("key_sc", keys_scales, COLS)
+        key_sc = load_scales("key_sc", keys_scales, COLS, nc.sync)
         key_w = load_words("key_w", keys_words[0], 2 * COLS)
         l_a = load_list("l_a", offs, HALF)
+        note_sc = load_scales("note_sc", notes_scales, COLS, nc.gpsimd)
+        note_w = load_words("note_w", notes_words[0].rearrange(flat), 4 * COLS)
+        l_b = load_list("l_b", offs2, HALF)
         q2_raw = load_query("q2", query2)
-        user_sc = load_scales("user_sc", users_scales, COLS)
+        user_sc = load_scales("user_sc", users_scales, COLS, nc.sync)
         user_w = load_words("user_w", users_words[0].rearrange(flat), 4 * COLS)
         l_c = load_list("l_c", offs3, SLOTS)
         l_put = load_list("l_put", offs4, SLOTS)
-        note_sc = load_scales("note_sc", notes_scales, COLS)
-        note_w = load_words("note_w", notes_words[0].rearrange(flat), 4 * COLS)
-        l_b = load_list("l_b", offs2, HALF)
         l_g = load_list("l_g", offs5, SLOTS)
         row_f = keep.tile([P, PACK], F32, name="row_f")
         nc.sync.dma_start(row_f[:], rowf.rearrange("(p t) o -> p (t o)", t=PACK))
         mix_w = load_words("mix_w", mix_words[0].rearrange(flat), 4 * E)
-        mix_sc = load_scales("mix_sc", mix_scales, E)
+        mix_sc = load_scales("mix_sc", mix_scales, E, nc.sync)
 
         placed = [keep.tile([P, COLS], F32, name="placed%d" % k) for k in range(2)]
         for tile in placed:
             nc.vector.memset(tile[:], 0.0)
 
-        def quantise_query(name, raws):
+        def quantise_query(name, raws, copiers):
             dealt = keep.tile([P, PACK, P, PACK], BF16, name=name + "_dealt", align_bytes=64)
             codes = keep.tile([P, Q], U32, name=name + "_codes", align_bytes=64)
             scales = keep.tile([P, Q], U8, name=name + "_scales", align_bytes=64)
-            per = P // CHUNKS
             for c, raw in enumerate(raws):
-                nc.vector.tensor_copy(
-                    dealt[:, :, c * per : (c + 1) * per, :].rearrange("p t m j -> p m j t"),
+                copiers[c](
+                    dealt[:, :, :, 2 * c : 2 * c + 2].rearrange("p t m j -> p m j t"),
                     raw[:].rearrange("p j (m t) -> p m j t", t=PACK),
                 )
-            for t in range(PACK):
-                cols = slice(t * P, (t + 1) * P)
+            for lo, hi in ((0, 1), (1, PACK)):
+                cols = slice(lo * P, hi * P)
                 nc.vector.quantize_mx(
                     out=codes[:, cols].bitcast(FP8X4), scales=scales[:, cols],
-                    in_=dealt[:, t].rearrange("p m j -> p (m j)"),
+                    in_=dealt[:, lo:hi].rearrange("p t m j -> p (t m j)"),
                 )
             return codes, scales
 
-        def scores(name, tag, t, quantised, words, plane, dtype, copiers):
+        def scores(whole, t, quantised, words, plane, dtype, copiers):
             codes, scales = quantised
             cols = slice(t * P, (t + 1) * P)
             nbytes = words.shape[1] // COLS
-            whole = keep.tile([P, COLS], F32, name="%s%d" % (name, t))
             for h in range(COLS // BANK):
-                bank = psum.tile([P, BANK], F32, name=tag)
+                bank = next_bank()
                 nc.tensor.matmul_mx(
                     out=bank[:], lhsT=codes[:, cols].bitcast(FP8X4), lhsT_scale=scales[:, cols],
                     rhs=words[:, h * BANK * nbytes : (h + 1) * BANK * nbytes].bitcast(dtype),
@@ -129,67 +132,84 @@ def tile_attend_joinedbest_threeq_mixed_kernel(
         w = [keep.tile([P, SLOTS], F32, name="w%d" % t) for t in range(PACK)]
         c_pick = [keep.tile([P, SLOTS], F32, name="c_pick%d" % t) for t in range(PACK)]
         v = [keep.tile([P, SLOTS], F32, name="v%d" % t) for t in range(PACK)]
+        a_all = [keep.tile([P, COLS], F32, name="a_all%d" % t) for t in range(PACK)]
+        b_all = [keep.tile([P, COLS], F32, name="b_all%d" % t) for t in range(PACK)]
+        c_all = [keep.tile([P, COLS], F32, name="c_all%d" % t) for t in range(PACK)]
         cc = [keep.tile([P, COLS], F32, name="cc%d" % t) for t in range(PACK)]
         g = [keep.tile([P, SLOTS], F32, name="g%d" % t) for t in range(PACK)]
-        gw = keep.tile([P, PACK, SLOTS], BF16, name="gw")
+        pairs = keep.tile([P, 2, SLOTS, 2], BF16, name="pairs")
 
-        qq = quantise_query("q", q_raw)
+        qq = quantise_query("q", q_raw, (s_copy, v_copy))
 
         def tokens(t):
-            a = scores("a", "ab_bank", t, qq, key_w, key_sc, FP4X4, (s_copy, v_copy if t == 0 else s_copy))
+            a = scores(a_all[t], t, qq, key_w, key_sc, FP4X4, (s_copy, s_copy))
             s_gather(w[t][:, :HALF], a, l_a[:])
 
         def notes(t):
-            b = scores("b", "ab_bank", t, qq, note_w, note_sc, FP8X4, (s_copy, s_copy))
+            b = scores(b_all[t], t, qq, note_w, note_sc, FP8X4, (s_copy, s_copy))
             s_gather(w[t][:, HALF:], b, l_b[:])
 
-        def put(t, c0, lo, hi):
-            (v_gather if t == 2 else s_gather)(c_pick[t][:, lo:hi], c0, part(l_c, lo, hi))
+        def pick(gather, t, lo, hi):
+            gather(c_pick[t][:, lo:hi], c_all[t], part(l_c, lo, hi))
+
+        def put(t, lo, hi):
             nc.vector.tensor_tensor(v[t][:, lo:hi], w[t][:, lo:hi], c_pick[t][:, lo:hi], ALU.max)
             nc.vector.tensor_copy(placed[t % 2][:].indirect(part(l_put, lo, hi)), v[t][:, lo:hi])
 
         tokens(0)
+        notes(0)
         tokens(1)
-        qq2 = quantise_query("q2", q2_raw)
+        qq2 = quantise_query("q2", q2_raw, (v_copy, v_copy))
 
         for t in range(PACK):
+            if t >= 2:
+                tokens(t)
+            if t >= 1:
+                notes(t)
+            copier = v_copy if t == 0 else s_copy
+            c0 = scores(c_all[t], t, qq2, user_w, user_sc, FP8X4, (copier, copier))
             if t == 0:
-                c0 = scores("c", "c_bank", t, qq2, user_w, user_sc, FP8X4, (s_copy, v_copy))
-                put(t, c0, 0, HALF)
-                notes(t)
-                put(t, c0, HALF, SLOTS)
+                pick(v_gather, t, 0, HALF)
+                pick(s_gather, t, HALF, SLOTS)
             else:
-                if t >= 2:
-                    tokens(t)
-                c0 = scores("c", "c_bank", t, qq2, user_w, user_sc, FP8X4, (s_copy, s_copy))
-                notes(t)
-                put(t, c0, 0, SLOTS)
-            nc.vector.tensor_tensor(cc[t][:], c0[:], placed[t % 2][:], ALU.add)
+                pick(s_gather if t == PACK - 1 else v_gather, t, 0, SLOTS)
+            put(t, 0, SLOTS)
+            (nc.vector if t == PACK - 1 else nc.gpsimd).tensor_tensor(cc[t][:], c0[:], placed[t % 2][:], ALU.add)
+
+        def s_scale(t, lo, hi):
+            nc.scalar.activation(pairs[:, t // 2, lo:hi, t % 2], g[t][:, lo:hi], COPY, scale=row_f[:, t : t + 1])
+
+        def v_scale(t, lo, hi):
+            nc.vector.tensor_scalar(pairs[:, t // 2, lo:hi, t % 2], g[t][:, lo:hi], row_f[:, t : t + 1], None, ALU.mult)
 
         last = PACK - 1
         for t in range(last):
             s_gather(g[t][:], cc[t], l_g[:])
             if t < 2:
-                nc.scalar.activation(gw[:, t, :], g[t][:], COPY, scale=row_f[:, t : t + 1])
+                nc.gpsimd.tensor_scalar(pairs[:, 0, :, t], g[t][:], row_f[:, t : t + 1], 0.0, ALU.mult, ALU.add)
             else:
-                nc.vector.tensor_scalar(gw[:, t, :], g[t][:], row_f[:, t : t + 1], None, ALU.mult)
-        s_gather(g[last][:, HALF:], cc[last], part(l_g, HALF, SLOTS))
+                v_scale(t, 0, HALF)
+                s_scale(t, HALF, SLOTS)
         v_gather(g[last][:, :HALF], cc[last], part(l_g, 0, HALF))
+        s_gather(g[last][:, HALF:], cc[last], part(l_g, HALF, SLOTS))
+        v_scale(last, 0, HALF)
+        s_scale(last, HALF, SLOTS)
         out_rows = out.rearrange("(u p) i -> p u i", p=P)
+        pair_words = pairs[:].rearrange("p u i t -> p u (i t)").bitcast(I32)
+        woven = [keep.tile([P, HALF * PACK], BF16, name="woven%d" % h, align_bytes=64) for h in range(2)]
+        for h in range(2):
+            nc.vector.tensor_copy(
+                woven[h][:].bitcast(I32).rearrange("p (c i u) -> p c u i", i=4, u=2),
+                pair_words[:, :, h * HALF : (h + 1) * HALF].rearrange("p u (c i) -> p c u i", i=4),
+            )
         for h in range(2):
             slots = slice(h * HALF, (h + 1) * HALF)
-            nc.vector.tensor_scalar(gw[:, last, slots], g[last][:, slots], row_f[:, last : last + 1], None, ALU.mult)
-            woven = keep.tile([P, HALF, PACK], BF16, name="woven%d" % h, align_bytes=64)
-            nc.vector.tensor_copy(
-                woven[:].rearrange("p (c i) t -> p c t i", i=4),
-                gw[:, :, slots].rearrange("p t (c i) -> p c t i", i=4),
-            )
             gw_codes = keep.tile([P, HALF], U32, name="gw_codes%d" % h, align_bytes=64)
             gw_scales = keep.tile([P, HALF], U8, name="gw_scales%d" % h, align_bytes=64)
             nc.vector.quantize_mx(
-                out=gw_codes[:].bitcast(FP8X4), scales=gw_scales[:], in_=woven[:].rearrange("p i t -> p (i t)")
+                out=gw_codes[:].bitcast(FP8X4), scales=gw_scales[:], in_=woven[h][:]
             )
-            bank = psum.tile([P, BANK], F32, name="c_bank")
+            bank = next_bank()
             for u in range(E // P):
                 nc.tensor.matmul_mx(
                     out=bank[:, u * HALF : (u + 1) * HALF],
@@ -197,5 +217,5 @@ def tile_attend_joinedbest_threeq_mixed_kernel(
                     rhs=gw_codes[:].bitcast(FP8X4), rhs_scale=gw_scales[:], start=True, stop=True,
                 )
             result = keep.tile([P, E // P, HALF], F32, name="result%d" % h)
-            nc.scalar.copy(result[:].rearrange("p u i -> p (u i)"), bank[:])
+            (s_copy, v_copy)[h](result[:].rearrange("p u i -> p (u i)"), bank[:])
             nc.sync.dma_start(out_rows[:, :, slots], result[:])

@@ -19,7 +19,7 @@ D, Q, COLS, SLOTS, E = 512, 512, 1024, 512, 256
 HALF = SLOTS // 2
 BANK = 512
 LIST = 16
-RING = 4
+RING = 3
 
 FLOPS = 2 * D * Q * COLS * 3 + 2 * Q * E * SLOTS
 
@@ -39,14 +39,10 @@ def tile_attend_joinedbest_threeq_mixed_kernel(
             used.append(1)
             return banks[(len(used) - 1) % RING]
 
-        def load_query(name, src):
-            rows = src.rearrange("(p j) q -> p j q", j=PACK)
-            raws = []
-            for c in range(2):
-                raw = keep.tile([P, 2, Q], F32, name="%s_raw%d" % (name, c))
-                nc.sync.dma_start(raw[:], rows[:, 2 * c : 2 * c + 2, :])
-                raws.append(raw)
-            return raws
+        def load_rows(name, src, c):
+            raw = keep.tile([P, 2, Q], F32, name="%s_raw%d" % (name, c))
+            nc.sync.dma_start(raw[:], src.rearrange("(p j) q -> p j q", j=PACK)[:, 2 * c : 2 * c + 2, :])
+            return raw
 
         def load_scales(name, src, width, queue):
             plane = keep.tile([P, width], U8, name=name, align_bytes=64)
@@ -66,18 +62,19 @@ def tile_attend_joinedbest_threeq_mixed_kernel(
             return lst
 
         flat = "p n t -> p (n t)"
-        q_raw = load_query("q", query)
+        q_raw = [load_rows("q", query, c) for c in range(2)]
         key_sc = load_scales("key_sc", keys_scales, COLS, nc.sync)
         key_w = load_words("key_w", keys_words[0], 2 * COLS)
         l_a = load_list("l_a", offs, HALF)
         note_sc = load_scales("note_sc", notes_scales, COLS, nc.gpsimd)
         note_w = load_words("note_w", notes_words[0].rearrange(flat), 4 * COLS)
         l_b = load_list("l_b", offs2, HALF)
-        q2_raw = load_query("q2", query2)
+        l_c = load_list("l_c", offs3, SLOTS)
+        q2_raw = [load_rows("q2", query2, 0)]
+        l_put = load_list("l_put", offs4, SLOTS)
+        q2_raw.append(load_rows("q2", query2, 1))
         user_sc = load_scales("user_sc", users_scales, COLS, nc.sync)
         user_w = load_words("user_w", users_words[0].rearrange(flat), 4 * COLS)
-        l_c = load_list("l_c", offs3, SLOTS)
-        l_put = load_list("l_put", offs4, SLOTS)
         l_g = load_list("l_g", offs5, SLOTS)
         row_f = keep.tile([P, PACK], F32, name="row_f")
         nc.sync.dma_start(row_f[:], rowf.rearrange("(p t) o -> p (t o)", t=PACK))
@@ -133,11 +130,11 @@ def tile_attend_joinedbest_threeq_mixed_kernel(
         c_pick = [keep.tile([P, SLOTS], F32, name="c_pick%d" % t) for t in range(PACK)]
         v = [keep.tile([P, SLOTS], F32, name="v%d" % t) for t in range(PACK)]
         a_all = [keep.tile([P, COLS], F32, name="a_all%d" % t) for t in range(PACK)]
-        b_all = [keep.tile([P, COLS], F32, name="b_all%d" % t) for t in range(PACK)]
+        b_all = [keep.tile([P, COLS], F32, name="b_all%d" % t, tag="b_all%d" % t) for t in range(PACK)]
         c_all = [keep.tile([P, COLS], F32, name="c_all%d" % t) for t in range(PACK)]
         cc = [keep.tile([P, COLS], F32, name="cc%d" % t) for t in range(PACK)]
-        g = [keep.tile([P, SLOTS], F32, name="g%d" % t) for t in range(PACK)]
-        pairs = keep.tile([P, 2, SLOTS, 2], BF16, name="pairs")
+        pairs = keep.tile([P, SLOTS, 2], BF16, name="pairs")
+        woven = [keep.tile([P, HALF, PACK], BF16, name="woven%d" % h, align_bytes=64) for h in range(2)]
 
         qq = quantise_query("q", q_raw, (s_copy, v_copy))
 
@@ -157,15 +154,11 @@ def tile_attend_joinedbest_threeq_mixed_kernel(
             nc.vector.tensor_copy(placed[t % 2][:].indirect(part(l_put, lo, hi)), v[t][:, lo:hi])
 
         tokens(0)
-        notes(0)
         tokens(1)
+        notes(0)
         qq2 = quantise_query("q2", q2_raw, (v_copy, v_copy))
 
         for t in range(PACK):
-            if t >= 2:
-                tokens(t)
-            if t >= 1:
-                notes(t)
             copier = v_copy if t == 0 else s_copy
             c0 = scores(c_all[t], t, qq2, user_w, user_sc, FP8X4, (copier, copier))
             if t == 0:
@@ -173,41 +166,48 @@ def tile_attend_joinedbest_threeq_mixed_kernel(
                 pick(s_gather, t, HALF, SLOTS)
             else:
                 pick(s_gather if t == PACK - 1 else v_gather, t, 0, SLOTS)
+            if t >= 2:
+                tokens(t)
+            if t >= 1:
+                notes(t)
             put(t, 0, SLOTS)
             (nc.vector if t == PACK - 1 else nc.gpsimd).tensor_tensor(cc[t][:], c0[:], placed[t % 2][:], ALU.add)
 
-        def s_scale(t, lo, hi):
-            nc.scalar.activation(pairs[:, t // 2, lo:hi, t % 2], g[t][:, lo:hi], COPY, scale=row_f[:, t : t + 1])
+        def v_scale(t):
+            nc.vector.tensor_scalar(woven[0][:, :, t], g[t][:, :HALF], row_f[:, t : t + 1], None, ALU.mult)
 
-        def v_scale(t, lo, hi):
-            nc.vector.tensor_scalar(pairs[:, t // 2, lo:hi, t % 2], g[t][:, lo:hi], row_f[:, t : t + 1], None, ALU.mult)
+        def s_scale(t):
+            nc.scalar.activation(woven[1][:, :, t], g[t][:, HALF:], COPY, scale=row_f[:, t : t + 1])
+
+        def pair_words(h, word):
+            dst = woven[h][:].rearrange("p i t -> p (i t)").bitcast(word).rearrange("p (i u) -> p i u", u=2)
+            src = pairs[:, h * HALF : (h + 1) * HALF, :].rearrange("p i t -> p (i t)").bitcast(word)
+            return dst[:, :, 0], src
 
         last = PACK - 1
+        g_first = keep.tile([P, 2, SLOTS], F32, name="g_first", tag="b_all%d" % last)
+        g_last = keep.tile([P, SLOTS], F32, name="g_last")
+        g = [g_first[:, 0], g_first[:, 1], c_pick[last], g_last]
         for t in range(last):
-            s_gather(g[t][:], cc[t], l_g[:])
+            s_gather(g[t][:, :], cc[t], l_g[:])
             if t < 2:
-                nc.gpsimd.tensor_scalar(pairs[:, 0, :, t], g[t][:], row_f[:, t : t + 1], 0.0, ALU.mult, ALU.add)
+                nc.gpsimd.tensor_scalar(pairs[:, :, t], g[t][:, :], row_f[:, t : t + 1], 0.0, ALU.mult, ALU.add)
             else:
-                v_scale(t, 0, HALF)
-                s_scale(t, HALF, SLOTS)
+                v_scale(t)
+                s_scale(t)
+        s_copy(*pair_words(0, U32))
         v_gather(g[last][:, :HALF], cc[last], part(l_g, 0, HALF))
         s_gather(g[last][:, HALF:], cc[last], part(l_g, HALF, SLOTS))
-        v_scale(last, 0, HALF)
-        s_scale(last, HALF, SLOTS)
+        v_scale(last)
+        s_scale(last)
+        v_copy(*pair_words(1, I32))
         out_rows = out.rearrange("(u p) i -> p u i", p=P)
-        pair_words = pairs[:].rearrange("p u i t -> p u (i t)").bitcast(I32)
-        woven = [keep.tile([P, HALF * PACK], BF16, name="woven%d" % h, align_bytes=64) for h in range(2)]
-        for h in range(2):
-            nc.vector.tensor_copy(
-                woven[h][:].bitcast(I32).rearrange("p (c i u) -> p c u i", i=4, u=2),
-                pair_words[:, :, h * HALF : (h + 1) * HALF].rearrange("p u (c i) -> p c u i", i=4),
-            )
         for h in range(2):
             slots = slice(h * HALF, (h + 1) * HALF)
             gw_codes = keep.tile([P, HALF], U32, name="gw_codes%d" % h, align_bytes=64)
             gw_scales = keep.tile([P, HALF], U8, name="gw_scales%d" % h, align_bytes=64)
             nc.vector.quantize_mx(
-                out=gw_codes[:].bitcast(FP8X4), scales=gw_scales[:], in_=woven[h][:]
+                out=gw_codes[:].bitcast(FP8X4), scales=gw_scales[:], in_=woven[h][:].rearrange("p i t -> p (i t)")
             )
             bank = next_bank()
             for u in range(E // P):

@@ -19,7 +19,8 @@ D, Q, COLS, SLOTS, E = 512, 512, 1024, 512, 256
 HALF = SLOTS // 2
 BANK = 512
 LIST = 16
-RING = 3
+RING = 4
+V_ROWS = 80
 
 FLOPS = 2 * D * Q * COLS * 3 + 2 * Q * E * SLOTS
 
@@ -33,15 +34,16 @@ def tile_attend_joinedbest_threeq_mixed_kernel(
         keep = ctx.enter_context(tc.tile_pool(name="keep", bufs=1))
         psum = ctx.enter_context(tc.psum_pool(name="psum", bufs=1))
         banks = [psum.tile([P, BANK], F32, name="bank%d" % k) for k in range(RING)]
+        held = [psum.tile([P, BANK], F32, name="held%d" % k) for k in range(COLS // BANK)]
         used = []
 
         def next_bank():
             used.append(1)
             return banks[(len(used) - 1) % RING]
 
-        def load_rows(name, src, c):
-            raw = keep.tile([P, 2, Q], F32, name="%s_raw%d" % (name, c))
-            nc.sync.dma_start(raw[:], src.rearrange("(p j) q -> p j q", j=PACK)[:, 2 * c : 2 * c + 2, :])
+        def load_rows(name, src):
+            raw = keep.tile([P, PACK, Q], F32, name=name + "_raw")
+            nc.sync.dma_start(raw[:], src.rearrange("(p j) q -> p j q", j=PACK))
             return raw
 
         def load_scales(name, src, width, queue):
@@ -62,19 +64,18 @@ def tile_attend_joinedbest_threeq_mixed_kernel(
             return lst
 
         flat = "p n t -> p (n t)"
-        q_raw = [load_rows("q", query, c) for c in range(2)]
+        q_raw = load_rows("q", query)
         key_sc = load_scales("key_sc", keys_scales, COLS, nc.sync)
         key_w = load_words("key_w", keys_words[0], 2 * COLS)
         l_a = load_list("l_a", offs, HALF)
+        q2_raw = load_rows("q2", query2)
         note_sc = load_scales("note_sc", notes_scales, COLS, nc.gpsimd)
         note_w = load_words("note_w", notes_words[0].rearrange(flat), 4 * COLS)
-        l_b = load_list("l_b", offs2, HALF)
         l_c = load_list("l_c", offs3, SLOTS)
-        q2_raw = [load_rows("q2", query2, 0)]
         l_put = load_list("l_put", offs4, SLOTS)
-        q2_raw.append(load_rows("q2", query2, 1))
-        user_sc = load_scales("user_sc", users_scales, COLS, nc.sync)
         user_w = load_words("user_w", users_words[0].rearrange(flat), 4 * COLS)
+        user_sc = load_scales("user_sc", users_scales, COLS, nc.sync)
+        l_b = load_list("l_b", offs2, HALF)
         l_g = load_list("l_g", offs5, SLOTS)
         row_f = keep.tile([P, PACK], F32, name="row_f")
         nc.sync.dma_start(row_f[:], rowf.rearrange("(p t) o -> p (t o)", t=PACK))
@@ -85,14 +86,14 @@ def tile_attend_joinedbest_threeq_mixed_kernel(
         for tile in placed:
             nc.vector.memset(tile[:], 0.0)
 
-        def quantise_query(name, raws, copiers):
+        def quantise_query(name, raw, shares):
             dealt = keep.tile([P, PACK, P, PACK], BF16, name=name + "_dealt", align_bytes=64)
             codes = keep.tile([P, Q], U32, name=name + "_codes", align_bytes=64)
             scales = keep.tile([P, Q], U8, name=name + "_scales", align_bytes=64)
-            for c, raw in enumerate(raws):
-                copiers[c](
-                    dealt[:, :, :, 2 * c : 2 * c + 2].rearrange("p t m j -> p m j t"),
-                    raw[:].rearrange("p j (m t) -> p m j t", t=PACK),
+            for copier, lo, hi in shares:
+                copier(
+                    dealt[:, :, lo:hi, :].rearrange("p t m j -> p m j t"),
+                    raw[:, :, lo * PACK : hi * PACK].rearrange("p j (m t) -> p m j t", t=PACK),
                 )
             for lo, hi in ((0, 1), (1, PACK)):
                 cols = slice(lo * P, hi * P)
@@ -102,12 +103,12 @@ def tile_attend_joinedbest_threeq_mixed_kernel(
                 )
             return codes, scales
 
-        def scores(whole, t, quantised, words, plane, dtype, copiers):
+        def scores(whole, t, quantised, words, plane, dtype, copiers, into=None):
             codes, scales = quantised
             cols = slice(t * P, (t + 1) * P)
             nbytes = words.shape[1] // COLS
             for h in range(COLS // BANK):
-                bank = next_bank()
+                bank = into[h] if into else next_bank()
                 nc.tensor.matmul_mx(
                     out=bank[:], lhsT=codes[:, cols].bitcast(FP8X4), lhsT_scale=scales[:, cols],
                     rhs=words[:, h * BANK * nbytes : (h + 1) * BANK * nbytes].bitcast(dtype),
@@ -131,15 +132,14 @@ def tile_attend_joinedbest_threeq_mixed_kernel(
         v = [keep.tile([P, SLOTS], F32, name="v%d" % t) for t in range(PACK)]
         a_all = [keep.tile([P, COLS], F32, name="a_all%d" % t) for t in range(PACK)]
         b_all = [keep.tile([P, COLS], F32, name="b_all%d" % t, tag="b_all%d" % t) for t in range(PACK)]
-        c_all = [keep.tile([P, COLS], F32, name="c_all%d" % t) for t in range(PACK)]
         cc = [keep.tile([P, COLS], F32, name="cc%d" % t) for t in range(PACK)]
         pairs = keep.tile([P, SLOTS, 2], BF16, name="pairs")
         woven = [keep.tile([P, HALF, PACK], BF16, name="woven%d" % h, align_bytes=64) for h in range(2)]
 
-        qq = quantise_query("q", q_raw, (s_copy, v_copy))
+        qq = quantise_query("q", q_raw, ((v_copy, 0, V_ROWS), (s_copy, V_ROWS, P)))
 
         def tokens(t):
-            a = scores(a_all[t], t, qq, key_w, key_sc, FP4X4, (s_copy, s_copy))
+            a = scores(a_all[t], t, qq, key_w, key_sc, FP4X4, (s_copy, v_copy if t == 0 else s_copy))
             s_gather(w[t][:, :HALF], a, l_a[:])
 
         def notes(t):
@@ -156,22 +156,27 @@ def tile_attend_joinedbest_threeq_mixed_kernel(
         tokens(0)
         tokens(1)
         notes(0)
-        qq2 = quantise_query("q2", q2_raw, (v_copy, v_copy))
+        qq2 = quantise_query("q2", q2_raw, ((v_copy, 0, P),))
 
+        last = PACK - 1
+        c_all = []
         for t in range(PACK):
             copier = v_copy if t == 0 else s_copy
-            c0 = scores(c_all[t], t, qq2, user_w, user_sc, FP8X4, (copier, copier))
-            if t == 0:
-                pick(v_gather, t, 0, HALF)
-                pick(s_gather, t, HALF, SLOTS)
-            else:
-                pick(s_gather if t == PACK - 1 else v_gather, t, 0, SLOTS)
+            tag = "b_all%d" % (t - 1) if t == last else "c_all%d" % t
+            c_all.append(keep.tile([P, COLS], F32, name="c_all%d" % t, tag=tag))
+            scores(c_all[t], t, qq2, user_w, user_sc, FP8X4, (copier, copier), held if t == last else None)
+            pick(v_gather if t < 2 else s_gather, t, 0, SLOTS)
             if t >= 2:
                 tokens(t)
             if t >= 1:
                 notes(t)
             put(t, 0, SLOTS)
-            (nc.vector if t == PACK - 1 else nc.gpsimd).tensor_tensor(cc[t][:], c0[:], placed[t % 2][:], ALU.add)
+            if t < last:
+                nc.gpsimd.tensor_tensor(cc[t][:], c_all[t][:], placed[t % 2][:], ALU.add)
+            else:
+                for h, bank in enumerate(held):
+                    cols = slice(h * BANK, (h + 1) * BANK)
+                    nc.vector.tensor_tensor(cc[t][:, cols], bank[:], placed[t % 2][:, cols], ALU.add)
 
         def v_scale(t):
             nc.vector.tensor_scalar(woven[0][:, :, t], g[t][:, :HALF], row_f[:, t : t + 1], None, ALU.mult)
@@ -184,14 +189,16 @@ def tile_attend_joinedbest_threeq_mixed_kernel(
             src = pairs[:, h * HALF : (h + 1) * HALF, :].rearrange("p i t -> p (i t)").bitcast(word)
             return dst[:, :, 0], src
 
-        last = PACK - 1
         g_first = keep.tile([P, 2, SLOTS], F32, name="g_first", tag="b_all%d" % last)
         g_last = keep.tile([P, SLOTS], F32, name="g_last")
         g = [g_first[:, 0], g_first[:, 1], c_pick[last], g_last]
         for t in range(last):
             s_gather(g[t][:, :], cc[t], l_g[:])
             if t < 2:
-                nc.gpsimd.tensor_scalar(pairs[:, :, t], g[t][:, :], row_f[:, t : t + 1], 0.0, ALU.mult, ALU.add)
+                for lo in (0, HALF):
+                    nc.gpsimd.tensor_scalar(
+                        pairs[:, lo : lo + HALF, t], g[t][:, lo : lo + HALF], row_f[:, t : t + 1], 0.0, ALU.mult, ALU.add
+                    )
             else:
                 v_scale(t)
                 s_scale(t)
@@ -209,13 +216,13 @@ def tile_attend_joinedbest_threeq_mixed_kernel(
             nc.vector.quantize_mx(
                 out=gw_codes[:].bitcast(FP8X4), scales=gw_scales[:], in_=woven[h][:].rearrange("p i t -> p (i t)")
             )
-            bank = next_bank()
-            for u in range(E // P):
+            result = keep.tile([P, E // P, HALF], F32, name="result%d" % h)
+            for u, copier in enumerate((s_copy, v_copy)):
+                bank = next_bank()
                 nc.tensor.matmul_mx(
-                    out=bank[:, u * HALF : (u + 1) * HALF],
+                    out=bank[:, :HALF],
                     lhsT=mix_w[:, u * P * 4 : (u + 1) * P * 4].bitcast(FP8X4), lhsT_scale=mix_sc[:, u * P : (u + 1) * P],
                     rhs=gw_codes[:].bitcast(FP8X4), rhs_scale=gw_scales[:], start=True, stop=True,
                 )
-            result = keep.tile([P, E // P, HALF], F32, name="result%d" % h)
-            (s_copy, v_copy)[h](result[:].rearrange("p u i -> p (u i)"), bank[:])
+                copier(result[:, u, :], bank[:, :HALF])
             nc.sync.dma_start(out_rows[:, :, slots], result[:])

@@ -18,9 +18,11 @@ PACK = 4
 D, Q, COLS, SLOTS, E = 512, 512, 1024, 512, 256
 HALF = SLOTS // 2
 BANK = 512
+QUADRANT = 32
 LIST = 16
 RING = 4
 V_ROWS = 80
+V_PICKS = 2
 
 FLOPS = 2 * D * Q * COLS * 3 + 2 * Q * E * SLOTS
 
@@ -33,6 +35,7 @@ def tile_attend_joinedbest_threeq_mixed_kernel(
     with ExitStack() as ctx:
         keep = ctx.enter_context(tc.tile_pool(name="keep", bufs=1))
         psum = ctx.enter_context(tc.psum_pool(name="psum", bufs=1))
+
         banks = [psum.tile([P, BANK], F32, name="bank%d" % k) for k in range(RING)]
         held = [psum.tile([P, BANK], F32, name="held%d" % k) for k in range(COLS // BANK)]
         used = []
@@ -50,7 +53,7 @@ def tile_attend_joinedbest_threeq_mixed_kernel(
             plane = keep.tile([P, width], U8, name=name, align_bytes=64)
             rows = src[0].rearrange("(g r) n -> r g n", r=PACK)
             for r in range(PACK):
-                queue.dma_start(plane[r:P:32, :].bitcast(I32), rows[r].bitcast(I32))
+                queue.dma_start(plane[r:P:QUADRANT, :].bitcast(I32), rows[r].bitcast(I32))
             return plane
 
         def load_words(name, src, nbytes):
@@ -70,16 +73,16 @@ def tile_attend_joinedbest_threeq_mixed_kernel(
         l_a = load_list("l_a", offs, HALF)
         q2_raw = load_rows("q2", query2)
         note_sc = load_scales("note_sc", notes_scales, COLS, nc.gpsimd)
-        note_w = load_words("note_w", notes_words[0].rearrange(flat), 4 * COLS)
+        note_w = load_words("note_w", notes_words[0].rearrange(flat), PACK * COLS)
         l_c = load_list("l_c", offs3, SLOTS)
         l_put = load_list("l_put", offs4, SLOTS)
-        user_w = load_words("user_w", users_words[0].rearrange(flat), 4 * COLS)
+        user_w = load_words("user_w", users_words[0].rearrange(flat), PACK * COLS)
         user_sc = load_scales("user_sc", users_scales, COLS, nc.sync)
         l_b = load_list("l_b", offs2, HALF)
         l_g = load_list("l_g", offs5, SLOTS)
         row_f = keep.tile([P, PACK], F32, name="row_f")
         nc.sync.dma_start(row_f[:], rowf.rearrange("(p t) o -> p (t o)", t=PACK))
-        mix_w = load_words("mix_w", mix_words[0].rearrange(flat), 4 * E)
+        mix_w = load_words("mix_w", mix_words[0].rearrange(flat), PACK * E)
         mix_sc = load_scales("mix_sc", mix_scales, E, nc.sync)
 
         placed = [keep.tile([P, COLS], F32, name="placed%d" % k) for k in range(2)]
@@ -115,7 +118,6 @@ def tile_attend_joinedbest_threeq_mixed_kernel(
                     rhs_scale=plane[:, h * BANK : (h + 1) * BANK], start=True, stop=True,
                 )
                 copiers[h](whole[:, h * BANK : (h + 1) * BANK], bank[:])
-            return whole
 
         def part(lst, lo, hi):
             return lst[:, lo // LIST : hi // LIST]
@@ -133,25 +135,18 @@ def tile_attend_joinedbest_threeq_mixed_kernel(
         a_all = [keep.tile([P, COLS], F32, name="a_all%d" % t) for t in range(PACK)]
         b_all = [keep.tile([P, COLS], F32, name="b_all%d" % t, tag="b_all%d" % t) for t in range(PACK)]
         cc = [keep.tile([P, COLS], F32, name="cc%d" % t) for t in range(PACK)]
-        pairs = keep.tile([P, SLOTS, 2], BF16, name="pairs")
+        pairs = keep.tile([P, HALF, 2], BF16, name="pairs")
         woven = [keep.tile([P, HALF, PACK], BF16, name="woven%d" % h, align_bytes=64) for h in range(2)]
 
         qq = quantise_query("q", q_raw, ((v_copy, 0, V_ROWS), (s_copy, V_ROWS, P)))
 
         def tokens(t):
-            a = scores(a_all[t], t, qq, key_w, key_sc, FP4X4, (s_copy, v_copy if t == 0 else s_copy))
-            s_gather(w[t][:, :HALF], a, l_a[:])
+            scores(a_all[t], t, qq, key_w, key_sc, FP4X4, (s_copy, v_copy if t == 0 else s_copy))
+            s_gather(w[t][:, :HALF], a_all[t], l_a[:])
 
         def notes(t):
-            b = scores(b_all[t], t, qq, note_w, note_sc, FP8X4, (s_copy, s_copy))
-            s_gather(w[t][:, HALF:], b, l_b[:])
-
-        def pick(gather, t, lo, hi):
-            gather(c_pick[t][:, lo:hi], c_all[t], part(l_c, lo, hi))
-
-        def put(t, lo, hi):
-            nc.vector.tensor_tensor(v[t][:, lo:hi], w[t][:, lo:hi], c_pick[t][:, lo:hi], ALU.max)
-            nc.vector.tensor_copy(placed[t % 2][:].indirect(part(l_put, lo, hi)), v[t][:, lo:hi])
+            scores(b_all[t], t, qq, note_w, note_sc, FP8X4, (s_copy, s_copy))
+            s_gather(w[t][:, HALF:], b_all[t], l_b[:])
 
         tokens(0)
         tokens(1)
@@ -159,24 +154,25 @@ def tile_attend_joinedbest_threeq_mixed_kernel(
         qq2 = quantise_query("q2", q2_raw, ((v_copy, 0, P),))
 
         last = PACK - 1
-        c_all = []
         for t in range(PACK):
             copier = v_copy if t == 0 else s_copy
             tag = "b_all%d" % (t - 1) if t == last else "c_all%d" % t
-            c_all.append(keep.tile([P, COLS], F32, name="c_all%d" % t, tag=tag))
-            scores(c_all[t], t, qq2, user_w, user_sc, FP8X4, (copier, copier), held if t == last else None)
-            pick(v_gather if t < 2 else s_gather, t, 0, SLOTS)
+            c_all = keep.tile([P, COLS], F32, name="c_all%d" % t, tag=tag)
+            scores(c_all, t, qq2, user_w, user_sc, FP8X4, (copier, copier), held if t == last else None)
+            (v_gather if t < V_PICKS else s_gather)(c_pick[t][:, 0:SLOTS], c_all, part(l_c, 0, SLOTS))
             if t >= 2:
                 tokens(t)
             if t >= 1:
                 notes(t)
-            put(t, 0, SLOTS)
+            f1 = placed[t % 2]
+            nc.vector.tensor_tensor(v[t][:, 0:SLOTS], w[t][:, 0:SLOTS], c_pick[t][:, 0:SLOTS], ALU.max)
+            nc.vector.tensor_copy(f1[:].indirect(part(l_put, 0, SLOTS)), v[t][:, 0:SLOTS])
             if t < last:
-                nc.gpsimd.tensor_tensor(cc[t][:], c_all[t][:], placed[t % 2][:], ALU.add)
+                nc.gpsimd.tensor_tensor(cc[t][:], c_all[:], f1[:], ALU.add)
             else:
                 for h, bank in enumerate(held):
                     cols = slice(h * BANK, (h + 1) * BANK)
-                    nc.vector.tensor_tensor(cc[t][:, cols], bank[:], placed[t % 2][:, cols], ALU.add)
+                    nc.vector.tensor_tensor(cc[t][:, cols], bank[:], f1[:, cols], ALU.add)
 
         def v_scale(t):
             nc.vector.tensor_scalar(woven[0][:, :, t], g[t][:, :HALF], row_f[:, t : t + 1], None, ALU.mult)
@@ -184,31 +180,29 @@ def tile_attend_joinedbest_threeq_mixed_kernel(
         def s_scale(t):
             nc.scalar.activation(woven[1][:, :, t], g[t][:, HALF:], COPY, scale=row_f[:, t : t + 1])
 
-        def pair_words(h, word):
-            dst = woven[h][:].rearrange("p i t -> p (i t)").bitcast(word).rearrange("p (i u) -> p i u", u=2)
-            src = pairs[:, h * HALF : (h + 1) * HALF, :].rearrange("p i t -> p (i t)").bitcast(word)
-            return dst[:, :, 0], src
+        def g_scale(dst, t, lo):
+            nc.gpsimd.tensor_scalar(dst, g[t][:, lo : lo + HALF], row_f[:, t : t + 1], 0.0, ALU.mult, ALU.add)
 
         g_first = keep.tile([P, 2, SLOTS], F32, name="g_first", tag="b_all%d" % last)
         g_last = keep.tile([P, SLOTS], F32, name="g_last")
         g = [g_first[:, 0], g_first[:, 1], c_pick[last], g_last]
         for t in range(last):
             s_gather(g[t][:, :], cc[t], l_g[:])
-            if t < 2:
-                for lo in (0, HALF):
-                    nc.gpsimd.tensor_scalar(
-                        pairs[:, lo : lo + HALF, t], g[t][:, lo : lo + HALF], row_f[:, t : t + 1], 0.0, ALU.mult, ALU.add
-                    )
-            else:
-                v_scale(t)
-                s_scale(t)
-        s_copy(*pair_words(0, U32))
+        for t in range(2):
+            g_scale(pairs[:, :, t], t, 0)
+        for t in range(2):
+            g_scale(woven[1][:, :, t], t, HALF)
+        v_scale(2)
+        s_scale(2)
+        v_copy(
+            woven[0][:].rearrange("p i t -> p (i t)").bitcast(I32).rearrange("p (i u) -> p i u", u=2)[:, :, 0],
+            pairs[:].rearrange("p i t -> p (i t)").bitcast(I32),
+        )
         v_gather(g[last][:, :HALF], cc[last], part(l_g, 0, HALF))
         s_gather(g[last][:, HALF:], cc[last], part(l_g, HALF, SLOTS))
         v_scale(last)
         s_scale(last)
-        v_copy(*pair_words(1, I32))
-        out_rows = out.rearrange("(u p) i -> p u i", p=P)
+
         for h in range(2):
             slots = slice(h * HALF, (h + 1) * HALF)
             gw_codes = keep.tile([P, HALF], U32, name="gw_codes%d" % h, align_bytes=64)
@@ -221,8 +215,9 @@ def tile_attend_joinedbest_threeq_mixed_kernel(
                 bank = next_bank()
                 nc.tensor.matmul_mx(
                     out=bank[:, :HALF],
-                    lhsT=mix_w[:, u * P * 4 : (u + 1) * P * 4].bitcast(FP8X4), lhsT_scale=mix_sc[:, u * P : (u + 1) * P],
+                    lhsT=mix_w[:, u * P * PACK : (u + 1) * P * PACK].bitcast(FP8X4),
+                    lhsT_scale=mix_sc[:, u * P : (u + 1) * P],
                     rhs=gw_codes[:].bitcast(FP8X4), rhs_scale=gw_scales[:], start=True, stop=True,
                 )
                 copier(result[:, u, :], bank[:, :HALF])
-            nc.sync.dma_start(out_rows[:, :, slots], result[:])
+                nc.sync.dma_start(out[u * P : (u + 1) * P, slots], result[:, u, :])

from contextlib import ExitStack

import concourse.mybir as mybir

F32 = mybir.dt.float32
BF16 = mybir.dt.bfloat16
I32 = mybir.dt.int32
U32 = mybir.dt.uint32
U16 = mybir.dt.uint16
U8 = mybir.dt.uint8
FP8X4 = mybir.dt.float8_e4m3fn_x4
FP4X4 = mybir.dt.float4_e2m1fn_x4
COPY = mybir.ActivationFunctionType.Copy
ALU = mybir.AluOpType

P = 128
PACK = 4
D, Q, COLS, SLOTS, E = 512, 512, 1024, 512, 256
HALF = SLOTS // 2
BANK = 512
QUADRANT = 32
LIST = 16
RING = 4
V_ROWS = 80
V_PICKS = 2

FLOPS = 2 * D * Q * COLS * 3 + 2 * Q * E * SLOTS


def tile_attend_joinedbest_threeq_mixed_kernel(
    tc, query, query2, keys_words, keys_scales, notes_words, notes_scales, users_words, users_scales,
    rowf, mix_words, mix_scales, offs, offs2, offs3, offs4, offs5, out,
):
    nc = tc.nc
    with ExitStack() as ctx:
        keep = ctx.enter_context(tc.tile_pool(name="keep", bufs=1))
        psum = ctx.enter_context(tc.psum_pool(name="psum", bufs=1))

        banks = [psum.tile([P, BANK], F32, name="bank%d" % k) for k in range(RING)]
        held = [psum.tile([P, BANK], F32, name="held%d" % k) for k in range(COLS // BANK)]
        used = []

        def next_bank():
            used.append(1)
            return banks[(len(used) - 1) % RING]

        def load_rows(name, src):
            raw = keep.tile([P, PACK, Q], F32, name=name + "_raw")
            nc.sync.dma_start(raw[:], src.rearrange("(p j) q -> p j q", j=PACK))
            return raw

        def load_scales(name, src, width, queue):
            plane = keep.tile([P, width], U8, name=name, align_bytes=64)
            rows = src[0].rearrange("(g r) n -> r g n", r=PACK)
            for r in range(PACK):
                queue.dma_start(plane[r:P:QUADRANT, :].bitcast(I32), rows[r].bitcast(I32))
            return plane

        def load_words(name, src, nbytes):
            words = keep.tile([P, nbytes], U8, name=name, align_bytes=64)
            nc.sync.dma_start(words[:].bitcast(I32), src.bitcast(I32))
            return words

        def load_list(name, src, n):
            lst = keep.tile([P, n // LIST], U16, name=name)
            nc.sync.dma_start(lst[:], src)
            return lst

        flat = "p n t -> p (n t)"
        q_raw = load_rows("q", query)
        key_sc = load_scales("key_sc", keys_scales, COLS, nc.sync)
        key_w = load_words("key_w", keys_words[0], 2 * COLS)
        l_a = load_list("l_a", offs, HALF)
        q2_raw = load_rows("q2", query2)
        note_sc = load_scales("note_sc", notes_scales, COLS, nc.gpsimd)
        note_w = load_words("note_w", notes_words[0].rearrange(flat), PACK * COLS)
        l_c = load_list("l_c", offs3, SLOTS)
        l_put = load_list("l_put", offs4, SLOTS)
        user_w = load_words("user_w", users_words[0].rearrange(flat), PACK * COLS)
        user_sc = load_scales("user_sc", users_scales, COLS, nc.sync)
        l_b = load_list("l_b", offs2, HALF)
        l_g = load_list("l_g", offs5, SLOTS)
        row_f = keep.tile([P, PACK], F32, name="row_f")
        nc.sync.dma_start(row_f[:], rowf.rearrange("(p t) o -> p (t o)", t=PACK))
        mix_w = load_words("mix_w", mix_words[0].rearrange(flat), PACK * E)
        mix_sc = load_scales("mix_sc", mix_scales, E, nc.sync)

        placed = [keep.tile([P, COLS], F32, name="placed%d" % k) for k in range(2)]
        for tile in placed:
            nc.vector.memset(tile[:], 0.0)

        def quantise_query(name, raw, shares):
            dealt = keep.tile([P, PACK, P, PACK], BF16, name=name + "_dealt", align_bytes=64)
            codes = keep.tile([P, Q], U32, name=name + "_codes", align_bytes=64)
            scales = keep.tile([P, Q], U8, name=name + "_scales", align_bytes=64)
            for copier, lo, hi in shares:
                copier(
                    dealt[:, :, lo:hi, :].rearrange("p t m j -> p m j t"),
                    raw[:, :, lo * PACK : hi * PACK].rearrange("p j (m t) -> p m j t", t=PACK),
                )
            for lo, hi in ((0, 1), (1, PACK)):
                cols = slice(lo * P, hi * P)
                nc.vector.quantize_mx(
                    out=codes[:, cols].bitcast(FP8X4), scales=scales[:, cols],
                    in_=dealt[:, lo:hi].rearrange("p t m j -> p (t m j)"),
                )
            return codes, scales

        def scores(whole, t, quantised, words, plane, dtype, copiers, into=None):
            codes, scales = quantised
            cols = slice(t * P, (t + 1) * P)
            nbytes = words.shape[1] // COLS
            for h in range(COLS // BANK):
                bank = into[h] if into else next_bank()
                nc.tensor.matmul_mx(
                    out=bank[:], lhsT=codes[:, cols].bitcast(FP8X4), lhsT_scale=scales[:, cols],
                    rhs=words[:, h * BANK * nbytes : (h + 1) * BANK * nbytes].bitcast(dtype),
                    rhs_scale=plane[:, h * BANK : (h + 1) * BANK], start=True, stop=True,
                )
                copiers[h](whole[:, h * BANK : (h + 1) * BANK], bank[:])

        def part(lst, lo, hi):
            return lst[:, lo // LIST : hi // LIST]

        def s_gather(dst, window, offsets):
            nc.scalar.activation(dst, window[:].indirect(offsets), COPY)

        def v_gather(dst, window, offsets):
            nc.vector.tensor_copy(dst, window[:].indirect(offsets))

        s_copy, v_copy = nc.scalar.copy, nc.vector.tensor_copy
        w = [keep.tile([P, SLOTS], F32, name="w%d" % t) for t in range(PACK)]
        c_pick = [keep.tile([P, SLOTS], F32, name="c_pick%d" % t) for t in range(PACK)]
        v = [keep.tile([P, SLOTS], F32, name="v%d" % t) for t in range(PACK)]
        a_all = [keep.tile([P, COLS], F32, name="a_all%d" % t) for t in range(PACK)]
        b_all = [keep.tile([P, COLS], F32, name="b_all%d" % t, tag="b_all%d" % t) for t in range(PACK)]
        cc = [keep.tile([P, COLS], F32, name="cc%d" % t) for t in range(PACK)]
        pairs = keep.tile([P, HALF, 2], BF16, name="pairs")
        woven = [keep.tile([P, HALF, PACK], BF16, name="woven%d" % h, align_bytes=64) for h in range(2)]

        qq = quantise_query("q", q_raw, ((v_copy, 0, V_ROWS), (s_copy, V_ROWS, P)))

        def tokens(t):
            scores(a_all[t], t, qq, key_w, key_sc, FP4X4, (s_copy, v_copy if t == 0 else s_copy))
            s_gather(w[t][:, :HALF], a_all[t], l_a[:])

        def notes(t):
            scores(b_all[t], t, qq, note_w, note_sc, FP8X4, (s_copy, s_copy))
            s_gather(w[t][:, HALF:], b_all[t], l_b[:])

        tokens(0)
        tokens(1)
        notes(0)
        qq2 = quantise_query("q2", q2_raw, ((v_copy, 0, P),))

        last = PACK - 1
        for t in range(PACK):
            copier = v_copy if t == 0 else s_copy
            tag = "b_all%d" % (t - 1) if t == last else "c_all%d" % t
            c_all = keep.tile([P, COLS], F32, name="c_all%d" % t, tag=tag)
            scores(c_all, t, qq2, user_w, user_sc, FP8X4, (copier, copier), held if t == last else None)
            (v_gather if t < V_PICKS else s_gather)(c_pick[t][:, 0:SLOTS], c_all, part(l_c, 0, SLOTS))
            if t >= 2:
                tokens(t)
            if t >= 1:
                notes(t)
            f1 = placed[t % 2]
            nc.vector.tensor_tensor(v[t][:, 0:SLOTS], w[t][:, 0:SLOTS], c_pick[t][:, 0:SLOTS], ALU.max)
            nc.vector.tensor_copy(f1[:].indirect(part(l_put, 0, SLOTS)), v[t][:, 0:SLOTS])
            if t < last:
                nc.gpsimd.tensor_tensor(cc[t][:], c_all[:], f1[:], ALU.add)
            else:
                for h, bank in enumerate(held):
                    cols = slice(h * BANK, (h + 1) * BANK)
                    nc.vector.tensor_tensor(cc[t][:, cols], bank[:], f1[:, cols], ALU.add)

        def v_scale(t):
            nc.vector.tensor_scalar(woven[0][:, :, t], g[t][:, :HALF], row_f[:, t : t + 1], None, ALU.mult)

        def s_scale(t):
            nc.scalar.activation(woven[1][:, :, t], g[t][:, HALF:], COPY, scale=row_f[:, t : t + 1])

        def g_scale(dst, t, lo):
            nc.gpsimd.tensor_scalar(dst, g[t][:, lo : lo + HALF], row_f[:, t : t + 1], 0.0, ALU.mult, ALU.add)

        g_first = keep.tile([P, 2, SLOTS], F32, name="g_first", tag="b_all%d" % last)
        g_last = keep.tile([P, SLOTS], F32, name="g_last")
        g = [g_first[:, 0], g_first[:, 1], c_pick[last], g_last]
        for t in range(last):
            s_gather(g[t][:, :], cc[t], l_g[:])
        for t in range(2):
            g_scale(pairs[:, :, t], t, 0)
        for t in range(2):
            g_scale(woven[1][:, :, t], t, HALF)
        v_scale(2)
        s_scale(2)
        v_copy(
            woven[0][:].rearrange("p i t -> p (i t)").bitcast(I32).rearrange("p (i u) -> p i u", u=2)[:, :, 0],
            pairs[:].rearrange("p i t -> p (i t)").bitcast(I32),
        )
        v_gather(g[last][:, :HALF], cc[last], part(l_g, 0, HALF))
        s_gather(g[last][:, HALF:], cc[last], part(l_g, HALF, SLOTS))
        v_scale(last)
        s_scale(last)

        for h in range(2):
            slots = slice(h * HALF, (h + 1) * HALF)
            gw_codes = keep.tile([P, HALF], U32, name="gw_codes%d" % h, align_bytes=64)
            gw_scales = keep.tile([P, HALF], U8, name="gw_scales%d" % h, align_bytes=64)
            nc.vector.quantize_mx(
                out=gw_codes[:].bitcast(FP8X4), scales=gw_scales[:], in_=woven[h][:].rearrange("p i t -> p (i t)")
            )
            result = keep.tile([P, E // P, HALF], F32, name="result%d" % h)
            for u, copier in enumerate((s_copy, v_copy)):
                bank = next_bank()
                nc.tensor.matmul_mx(
                    out=bank[:, :HALF],
                    lhsT=mix_w[:, u * P * PACK : (u + 1) * P * PACK].bitcast(FP8X4),
                    lhsT_scale=mix_sc[:, u * P : (u + 1) * P],
                    rhs=gw_codes[:].bitcast(FP8X4), rhs_scale=gw_scales[:], start=True, stop=True,
                )
                copier(result[:, u, :], bank[:, :HALF])
                nc.sync.dma_start(out[u * P : (u + 1) * P, slots], result[:, u, :])
